import numpy as np
import ml_dtypes


def mxq(x, axis, fmt="e4m3"):
    dtype, down = {"e4m3": (ml_dtypes.float8_e4m3fn, 7), "e5m2": (ml_dtypes.float8_e5m2, 14)}[fmt]
    v = np.moveaxis(np.asarray(x, np.float32).astype(ml_dtypes.bfloat16).astype(np.float64), axis, -1)
    blocks = v.reshape(v.shape[:-1] + (-1, 32))
    amax = np.abs(blocks).max(-1, keepdims=True)
    byte = np.maximum(np.where(amax > 0, np.frexp(amax)[1] - 1 + 127, 0) - down, 1)
    scale = np.exp2(byte - 127.0)
    codes = (blocks / scale).astype(np.float32).astype(dtype).astype(np.float64)
    return np.moveaxis((codes * scale).reshape(v.shape), -1, axis)


WIDE = False


def mx_kscale(k):
    if not WIDE:
        return np.ones(k)
    levels = np.array([10, -10, 5, -5, 0])
    if k % 512:
        return np.exp2(np.random.permutation(np.resize(levels, k // 32))).repeat(32)
    a = np.empty((k // 512, 16))
    for p in range(k // 512):
        a[p, :8] = np.random.permutation(np.resize(levels, 8))
        for g in range(8):
            far = levels[np.abs(levels - a[p, g]) >= 10]
            a[p, g + 8] = far[np.random.randint(len(far))]
    return np.exp2(a.ravel()).repeat(32)


def f64(x):
    return np.asarray(x).astype(np.float64)


def striped(idx):
    return np.tile(idx.reshape(-1, 16).T, (8, 1)).astype(np.uint16)


def unstriped(offs):
    return offs[:16].T.reshape(-1).astype(np.int64)


E2M1 = np.array([0.0, 0.5, 1.0, 1.5, 2.0, 3.0, 4.0, 6.0, -0.0, -0.5, -1.0, -1.5, -2.0, -3.0, -4.0, -6.0])


def pack_weight(w, fmt):
    k, n = w.shape
    w = f64(np.asarray(w, np.float32).astype(ml_dtypes.bfloat16)).reshape(k // 32, 32, n)
    amax = np.abs(w).max(1)
    if fmt == "e4m3":
        byte = np.frexp(amax)[1] - 1 + 127 - 7
    else:
        mant, ex = np.frexp(amax / 6.0)
        byte = np.where(mant > 0.5, ex, ex - 1) + 127
    byte = np.clip(np.where(amax > 0, byte, 1), 1, 254)
    scaled = (w * np.exp2(127.0 - byte)[:, None, :]).reshape(k, n).astype(np.float32)
    by_word = np.ascontiguousarray(scaled.reshape(k // 512, 128, 4, n).transpose(0, 1, 3, 2))
    if fmt == "e4m3":
        words = by_word.astype(ml_dtypes.float8_e4m3fn).view(np.uint8)
    else:
        c = by_word.astype(ml_dtypes.float4_e2m1fn).view(np.uint8) & 0xF
        words = (c[..., 0::2] | (c[..., 1::2] << 4)).reshape(k // 512, 128, 2 * n)
    return np.ascontiguousarray(words), np.ascontiguousarray(byte.astype(np.uint8).reshape(k // 512, 16, n))


def unpack_weight(words, scales, fmt):
    g, _, n = scales.shape
    words = np.ascontiguousarray(words).reshape(g, 128, n, -1)
    if fmt == "e4m3":
        vals = words.view(ml_dtypes.float8_e4m3fn).astype(np.float64)
    else:
        nib = np.empty((g, 128, n, 4), np.uint8)
        nib[..., 0::2] = words & 0xF
        nib[..., 1::2] = words >> 4
        vals = E2M1[nib]
    vals = vals * np.repeat(np.exp2(scales.astype(np.float64) - 127.0), 8, axis=1)[..., None]
    return vals.transpose(0, 1, 3, 2).reshape(g * 512, n)


def gelu(v):
    return 0.5 * v * (1.0 + np.tanh(np.sqrt(2.0 / np.pi) * (v + 0.044715 * v**3)))


K, H, T, S, P = 1024, 512, 4096, 1024, 512


def setup_inputs():
    n = np.random.standard_normal
    s = mx_kscale(K)[:, None]
    u = mx_kscale(H)[:, None]
    tab_words, tab_scales = pack_weight(n((K, T)) * s, "e4m3")
    w2_words, w2_scales = pack_weight(1.5 * n((K, H)) / np.sqrt(K) / s, "e2m1")
    return {
        "tab_words": tab_words,
        "tab_scales": tab_scales,
        "offs": striped(np.random.permutation(T)[:S]),
        "pos1": striped(np.random.permutation(S)[:P]),
        "pos2": striped(np.random.permutation(S)[:P]),
        "w1": (n((K, H)) / np.sqrt(K) / s * u.T).astype(np.float32),
        "w2_words": w2_words,
        "w2_scales": w2_scales,
        "w3": (0.7 * n((K, H)) / np.sqrt(K) / s).astype(np.float32),
        "gain": (np.random.uniform(0.7, 1.9, H) / np.sqrt(H) / u[:, 0] ** 2).astype(np.float32),
        "cap": (0.6 + 0.5 * n(P)).astype(np.float32),
    }


def reference(tab_words, tab_scales, offs, pos1, pos2, w1, w2_words, w2_scales, w3, gain, cap):
    v = unpack_weight(tab_words, tab_scales, "e4m3")[:, unstriped(offs)]
    w2 = unpack_weight(w2_words, w2_scales, "e2m1")
    theme = mxq(f64(w1), 0, "e4m3").T @ v
    tone = w2.T @ v
    image = mxq(f64(w3), 0, "e4m3").T @ v
    h = theme * (np.tanh(tone) + image)
    x1 = h[:, unstriped(pos1)]
    x2 = np.abs(h[:, unstriped(pos2)]) * f64(gain)[:, None]
    e = mxq(x1, 0, "e4m3").T @ mxq(x2, 0, "e4m3")
    return np.exp(np.minimum(e, f64(cap)[:, None]))

@@ -1,0 +1,305 @@
+from contextlib import ExitStack
+
+import concourse.mybir as mybir
+from concourse.masks import make_identity
+
+K, H, T, S, PICK = 1024, 512, 4096, 1024, 512
+FLOPS = 2 * (3 * K * H * S + H * PICK * PICK)
+
+F32 = mybir.dt.float32
+BF16 = mybir.dt.bfloat16
+I32 = mybir.dt.int32
+U32 = mybir.dt.uint32
+U16 = mybir.dt.uint16
+U8 = mybir.dt.uint8
+FP8X4 = mybir.dt.float8_e4m3fn_x4
+FP4X4 = mybir.dt.float4_e2m1fn_x4
+ACT = mybir.ActivationFunctionType
+ALU = mybir.AluOpType
+
+P = 128
+PACK = 4
+PASSES = K // (P * PACK)
+BANK = 512
+HALVES = S // BANK
+BLOCKS = PICK // P
+LIST_ROWS = 16
+TAB1_AT = 4 * T
+PICK1_AT = 8 * T
+PICK2_AT = PICK1_AT + 4096
+W3_AT = PICK2_AT + 2048
+TAB_SC_AT = W3_AT + 7168
+
+
+def tile_list_proverb_kinship_scores_kernel(
+    tc, tab_words, tab_scales, offs, pos1, pos2, w1, w2_words, w2_scales, w3, gain, cap, out
+):
+    nc = tc.nc
+    with ExitStack() as ctx:
+        keep = ctx.enter_context(tc.tile_pool(name="keep", bufs=1))
+        shared = ctx.enter_context(tc.tile_pool(name="shared", bufs=1))
+        psum = ctx.enter_context(tc.psum_pool(name="psum", bufs=8))
+
+        def sb(shape, dtype, name, tag=None):
+            return keep.tile(shape, dtype, name=name, tag=tag or name, align_bytes=64)
+
+        def placed(shape, dtype, name, offset):
+            return shared.tile(shape, dtype, name=name, align_bytes=64, offset=offset)
+
+        def bank(name):
+            return psum.tile([P, BANK], F32, name=name, tag="bank")
+
+        offs_sb = sb([P, S // LIST_ROWS], U16, "offs_sb")
+        pos1_sb = sb([P, PICK // LIST_ROWS], U16, "pos1_sb")
+        pos2_sb = sb([P, PICK // LIST_ROWS], U16, "pos2_sb")
+
+        tab_sc = placed([P, T], U8, "tab_sc", TAB_SC_AT)
+        nc.vector.memset(tab_sc[:].bitcast(I32), 0)
+        for quad in range(4):
+            nc.gpsimd.dma_start(
+                out=tab_sc[32 * quad : 32 * quad + 4 * PASSES, :].bitcast(I32),
+                in_=tab_scales[:, 4 * quad : 4 * quad + 4, :].bitcast(I32),
+            )
+        w2_sc_raw = sb([P, PASSES * H], U8, "w2_sc_raw")
+        nc.vector.memset(w2_sc_raw[:].bitcast(I32), 0)
+        for quad in range(4):
+            nc.scalar.dma_start(
+                out=w2_sc_raw[32 * quad : 32 * quad + 4, :].bitcast(I32).rearrange("r (a c) -> r a c", a=PASSES),
+                in_=w2_scales[:, 4 * quad : 4 * quad + 4, :].bitcast(I32).rearrange("a r c -> r a c"),
+            )
+        v_sc1 = sb([P, S], U8, "v_sc1")
+        nc.vector.memset(v_sc1[:].bitcast(I32), 0)
+        ident = sb([P, P], F32, "ident")
+        make_identity(nc, ident[:])
+        rows = sb([P, P], F32, "rows")
+        nc.vector.memset(rows[:], 0.0)
+        nc.gpsimd.dma_start(
+            out=rows[0:PACK, :].rearrange("t (q e) -> t q e", e=4),
+            in_=gain.rearrange("(q t e) -> t q e", t=PACK, e=4),
+        )
+        nc.gpsimd.dma_start(out=rows[PACK : PACK + BLOCKS, :], in_=cap.rearrange("(b p) -> b p", p=P))
+
+        nc.sync.dma_start(offs_sb[:], offs)
+        tab = {}
+        raw = {}
+
+        def load_table(a, tile):
+            tab[a] = tile
+            nc.sync.dma_start(
+                out=tab[a][:].bitcast(I32), in_=tab_words[a].rearrange("p t i -> p (t i)").bitcast(I32)
+            )
+
+        def load_weight(name, w, a, tile):
+            raw[name, a] = tile
+            nc.sync.dma_start(
+                out=raw[name, a][:],
+                in_=w[a * P * PACK : (a + 1) * P * PACK, :].rearrange("(p j) r -> p j r", j=PACK),
+            )
+
+        load_table(0, placed([P, T], U32, "tab0", 0))
+        w2_raw = sb([P, PASSES * 2 * H], U8, "w2_raw")
+        nc.sync.dma_start(
+            out=w2_raw[:].bitcast(I32).rearrange("p (a c) -> p a c", a=PASSES),
+            in_=w2_words.bitcast(I32).rearrange("a p c -> p a c"),
+        )
+        load_table(1, placed([P, T], U32, "tab1", TAB1_AT))
+        nc.sync.dma_start(pos2_sb[:], pos2)
+        nc.sync.dma_start(pos1_sb[:], pos1)
+
+        w2_codes = sb([P, PASSES * 2 * H], U8, "w2_codes")
+        nc.vector.tensor_copy(
+            out=w2_codes[:].bitcast(I32).rearrange("p (a t q u) -> p a t q u", a=PASSES, t=PACK, u=2),
+            in_=w2_raw[:].bitcast(I32).rearrange("p (a q t u) -> p a t q u", a=PASSES, t=PACK, u=2),
+        )
+
+
+        cols = BANK // LIST_ROWS
+        v = {}
+        v0 = sb([P, S], U32, "v0")
+        nc.vector.tensor_copy(out=v0[:], in_=tab[0][:].indirect(offs_sb[:]))
+        load_weight("w3", w3, 0, placed([P, PACK, H], F32, "w3_raw0", 2 * T))
+        v_sc = placed([P, S], U8, "v_sc", 0)
+        nc.vector.tensor_copy(out=v_sc[:], in_=tab_sc[:].indirect(offs_sb[:]))
+        nc.scalar.dma_start(out=v_sc1[0:100, :].bitcast(I32), in_=v_sc[4:104, :].bitcast(I32))
+        packed_planes = [v_sc[:], v_sc[4:P, :]]
+        level_planes = [v_sc[:], v_sc1[:]]
+        load_weight("w3", w3, 1, placed([P, PACK, H], F32, "w3_raw1", W3_AT))
+
+        w2_sc = sb([P, PASSES * H], U8, "w2_sc")
+        nc.vector.tensor_copy(
+            out=w2_sc[:].bitcast(I32).rearrange("p (a t q) -> p a t q", a=PASSES, t=PACK),
+            in_=w2_sc_raw[:].bitcast(I32).rearrange("p (a q t) -> p a t q", a=PASSES, t=PACK),
+        )
+
+        for half in range(HALVES):
+            v[0, half] = v0[:, half * BANK : (half + 1) * BANK]
+        for half in range(HALVES):
+            v1 = placed([P, BANK], U32, f"v1_{half}", TAB_SC_AT + 1024 + 2048 * half)
+            nc.vector.tensor_copy(
+                out=v1[:], in_=tab[1][:].indirect(offs_sb[:, half * cols : (half + 1) * cols])
+            )
+            v[1, half] = v1[:]
+        load_weight("w1", w1, 0, placed([P, PACK, H], F32, "w1_raw0", TAB1_AT))
+
+        turned = bank("turned")
+        nc.tensor.transpose(turned[:, 0:P], rows[:], ident[:])
+        per_row = sb([P, PACK + BLOCKS], F32, "per_row")
+        nc.scalar.activation(out=per_row[:], in_=turned[:, 0 : PACK + BLOCKS], func=ACT.Copy)
+
+        def first_stage(name, operands, planes, t, half, order):
+            acc = bank(f"{name}_{t}_{half}")
+            for a in order:
+                codes, scales = operands[a, t]
+                nc.tensor.matmul_mx(
+                    out=acc[:],
+                    lhsT=codes,
+                    lhsT_scale=scales,
+                    rhs=v[a, half].bitcast(FP8X4),
+                    rhs_scale=planes[a][:, half * BANK : (half + 1) * BANK],
+                    start=(a == order[0]),
+                    stop=(a == order[-1]),
+                )
+            return acc
+
+        def cast(name, a, slots, copy, tag=None, offset=None):
+            n = len(slots)
+            if offset is None:
+                grouped = sb([P, n * P * PACK], BF16, f"{name}_bf{a}_{slots[0]}", tag=tag)
+            else:
+                grouped = placed([P, n * P * PACK], BF16, f"{name}_bf{a}_{slots[0]}", offset)
+            copy(
+                out=grouped[:].rearrange("p (t q e j) -> p t q j e", t=n, e=4, j=PACK),
+                in_=raw[name, a][:].rearrange("p j (q t e) -> p t q j e", t=PACK, e=4)[
+                    :, slots[0] : slots[0] + n
+                ],
+            )
+            return grouped
+
+        def quantise(name, grouped, tag=None):
+            width = grouped.shape[1] // PACK
+            codes = sb([P, width], U32, f"{name}_codes", tag=tag)
+            scales = sb([P, width], U8, f"{name}_scales")
+            nc.vector.quantize_mx(out=codes[:].bitcast(FP8X4), scales=scales[:], in_=grouped[:])
+            return codes, scales
+
+        def quantise_weight(name, a, slots, grouped, operands, tag=None):
+            codes, scales = quantise(f"{name}_{a}_{slots[0]}", grouped, tag)
+            for i, t in enumerate(slots):
+                operands[a, t] = (
+                    codes[:, i * P : (i + 1) * P].bitcast(FP8X4),
+                    scales[:, i * P : (i + 1) * P],
+                )
+
+        w2_ops = {}
+        for a in range(PASSES):
+            for t in range(PACK):
+                c0 = a * H + t * P
+                w2_ops[a, t] = (w2_codes[:, 2 * c0 : 2 * (c0 + P)].bitcast(FP4X4), w2_sc[:, c0 : c0 + P])
+        u = {}
+        bent = {}
+        for half in range(HALVES):
+            for t in range(PACK):
+                acc = first_stage("tone", w2_ops, level_planes, t, half, [0, 1])
+                bent[t, half] = sb([P, BANK], F32, f"bent_{t}_{half}")
+                nc.scalar.activation(out=bent[t, half][:], in_=acc[:], func=ACT.Tanh)
+
+        w3_ops = {}
+        every = [0, 1, 2, 3]
+        grouped = cast("w3", 0, every, nc.vector.tensor_copy, offset=TAB1_AT + 2 * T)
+        load_weight("w1", w1, 1, placed([P, PACK, H], F32, "w1_raw1", 2 * T))
+        quantise_weight("w3", 0, every, grouped, w3_ops)
+        pairs = [([0, 1], nc.vector.tensor_copy, None), ([2, 3], nc.vector.tensor_copy, None)]
+        for slots, copy, tag in pairs:
+            quantise_weight("w3", 1, slots, cast("w3", 1, slots, copy, tag), w3_ops)
+            for t in slots:
+                for half in range(HALVES):
+                    acc = first_stage("image", w3_ops, packed_planes, t, half, [1, 0])
+                    if (t, half) == (PACK - 1, HALVES - 1):
+                        u[t, half] = placed([P, BANK], F32, f"u_{t}_{half}", PICK1_AT + 1024)
+                    else:
+                        u[t, half] = sb([P, BANK], F32, f"u_{t}_{half}")
+                    nc.vector.tensor_tensor(out=u[t, half][:], in0=acc[:], in1=bent[t, half][:], op=ALU.add)
+
+        w1_ops = {}
+        quantise_weight("w1", 0, every, cast("w1", 0, every, nc.scalar.copy, "w2_codes"), w1_ops)
+        w1_last = [cast("w1", 1, [t], nc.scalar.copy) for t in range(PACK)]
+        quantise_weight("w1", 1, [0], w1_last[0], w1_ops)
+        quantise_weight("w1", 1, [1], w1_last[1], w1_ops)
+        h = []
+        x2_bf = sb([P, PICK * PACK], BF16, "x2_bf")
+        for t in range(PACK):
+            h.append(sb([P, S], F32, f"h{t}"))
+            for half in range(HALVES):
+                acc = first_stage("theme", w1_ops, packed_planes, t, half, [1, 0])
+                nc.vector.tensor_tensor(
+                    out=h[t][:, half * BANK : (half + 1) * BANK], in0=acc[:], in1=u[t, half][:], op=ALU.mult
+                )
+            if t + 2 < PACK:
+                quantise_weight("w1", 1, [t + 2], w1_last[t + 2], w1_ops, tag=f"u_{t}_0")
+            if t == PACK - 1:
+                picked2 = placed([P, PICK], F32, f"picked2_{t}", PICK2_AT)
+            else:
+                picked2 = sb([P, PICK], F32, f"picked2_{t}")
+            nc.vector.tensor_copy(out=picked2[:], in_=h[t][:].indirect(pos2_sb[:]))
+            nc.scalar.activation(out=picked2[:], in_=picked2[:], func=ACT.Abs)
+            nc.scalar.activation(
+                out=x2_bf[:].rearrange("p (j t) -> p t j", t=PACK)[:, t, :],
+                in_=picked2[:],
+                func=ACT.Copy,
+                scale=per_row[:, t : t + 1],
+            )
+
+        cols1 = P // LIST_ROWS
+        x1_bf = {}
+        scores = {}
+
+        def pick1(b):
+            picked1 = placed([P, PACK, P], F32, f"picked1_{b}", PICK1_AT + 2048 * (b % 2))
+            for t in range(PACK):
+                nc.vector.tensor_copy(
+                    out=picked1[:, t, :], in_=h[t][:].indirect(pos1_sb[:, b * cols1 : (b + 1) * cols1])
+                )
+            if b < 2:
+                x1_bf[b] = placed([P, P * PACK], BF16, f"x1_bf{b}", PICK2_AT + 1024 * b)
+            else:
+                x1_bf[b] = sb([P, P * PACK], BF16, f"x1_bf{b}")
+            nc.scalar.copy(
+                out=x1_bf[b][:].rearrange("p (c i t) -> p c t i", i=4, t=PACK),
+                in_=picked1[:].rearrange("p t (c i) -> p c t i", i=4),
+            )
+
+        def score(b):
+            x1_codes, x1_scales = quantise(f"x1_{b}", x1_bf[b])
+            scores[b] = bank(f"e_{b}")
+            nc.tensor.matmul_mx(
+                out=scores[b][:],
+                lhsT=x1_codes[:].bitcast(FP8X4),
+                lhsT_scale=x1_scales[:],
+                rhs=x2_codes[:].bitcast(FP8X4),
+                rhs_scale=x2_scales[:],
+                start=True,
+                stop=True,
+            )
+
+        def finish(b):
+            capped = sb([P, PICK], F32, f"capped{b}")
+            nc.vector.tensor_scalar(
+                out=capped[:],
+                in0=scores[b][:],
+                scalar1=per_row[:, PACK + b : PACK + b + 1],
+                scalar2=None,
+                op0=ALU.min,
+            )
+            nc.scalar.activation(out=capped[:], in_=capped[:], func=ACT.Exp)
+            nc.sync.dma_start(out=out[b * P : (b + 1) * P, :], in_=capped[:])
+
+        pick1(0)
+        pick1(1)
+        x2_codes, x2_scales = quantise("x2", x2_bf)
+        for b in range(BLOCKS + 1):
+            if b < BLOCKS:
+                score(b)
+            if b >= 1:
+                finish(b - 1)
+            if b + 2 < BLOCKS:
+                pick1(b + 2)

@@ -1,7 +1,6 @@
 from contextlib import ExitStack
 
 import concourse.mybir as mybir
-from concourse.masks import make_identity
 
 K, H, T, S, PICK = 1024, 512, 4096, 1024, 512
 FLOPS = 2 * (3 * K * H * S + H * PICK * PICK)
@@ -24,11 +23,12 @@ BANK = 512
 HALVES = S // BANK
 BLOCKS = PICK // P
 LIST_ROWS = 16
-TAB1_AT = 4 * T
-PICK1_AT = 8 * T
+W2_SC_AT = 8192
+W2_CODES_AT = 9216
+W3_LATE_AT = 11264
+TAB1_AT = W3_LATE_AT + 8192
+PICK1_AT = TAB1_AT + 4 * T
 PICK2_AT = PICK1_AT + 4096
-W3_AT = PICK2_AT + 2048
-TAB_SC_AT = W3_AT + 7168
 
 
 def tile_list_proverb_kinship_scores_kernel(
@@ -53,33 +53,16 @@ def tile_list_proverb_kinship_scores_kernel(
         pos1_sb = sb([P, PICK // LIST_ROWS], U16, "pos1_sb")
         pos2_sb = sb([P, PICK // LIST_ROWS], U16, "pos2_sb")
 
-        tab_sc = placed([P, T], U8, "tab_sc", TAB_SC_AT)
-        nc.vector.memset(tab_sc[:].bitcast(I32), 0)
-        for quad in range(4):
-            nc.gpsimd.dma_start(
-                out=tab_sc[32 * quad : 32 * quad + 4 * PASSES, :].bitcast(I32),
-                in_=tab_scales[:, 4 * quad : 4 * quad + 4, :].bitcast(I32),
-            )
+        tab_sc = sb([P, T], U8, "tab_sc")
+        nc.vector.memset(tab_sc[32:64, :].bitcast(I32), 0)
+        nc.vector.memset(tab_sc[64:P, :].bitcast(I32), 0)
         w2_sc_raw = sb([P, PASSES * H], U8, "w2_sc_raw")
-        nc.vector.memset(w2_sc_raw[:].bitcast(I32), 0)
-        for quad in range(4):
-            nc.scalar.dma_start(
-                out=w2_sc_raw[32 * quad : 32 * quad + 4, :].bitcast(I32).rearrange("r (a c) -> r a c", a=PASSES),
-                in_=w2_scales[:, 4 * quad : 4 * quad + 4, :].bitcast(I32).rearrange("a r c -> r a c"),
-            )
-        v_sc1 = sb([P, S], U8, "v_sc1")
-        nc.vector.memset(v_sc1[:].bitcast(I32), 0)
-        ident = sb([P, P], F32, "ident")
-        make_identity(nc, ident[:])
-        rows = sb([P, P], F32, "rows")
-        nc.vector.memset(rows[:], 0.0)
-        nc.gpsimd.dma_start(
-            out=rows[0:PACK, :].rearrange("t (q e) -> t q e", e=4),
-            in_=gain.rearrange("(q t e) -> t q e", t=PACK, e=4),
-        )
-        nc.gpsimd.dma_start(out=rows[PACK : PACK + BLOCKS, :], in_=cap.rearrange("(b p) -> b p", p=P))
+        nc.gpsimd.memset(w2_sc_raw[:].bitcast(I32), 0)
+        planes = []
+        for a in range(PASSES):
+            planes.append(sb([P, S], U8, f"plane{a}"))
+            nc.vector.memset(planes[a][:].bitcast(I32), 0)
 
-        nc.sync.dma_start(offs_sb[:], offs)
         tab = {}
         raw = {}
 
@@ -96,6 +79,15 @@ def tile_list_proverb_kinship_scores_kernel(
                 in_=w[a * P * PACK : (a + 1) * P * PACK, :].rearrange("(p j) r -> p j r", j=PACK),
             )
 
+        nc.sync.dma_start(offs_sb[:], offs)
+        nc.sync.dma_start(
+            out=tab_sc[0:32, :].bitcast(I32), in_=tab_scales.rearrange("a q t -> (a q) t").bitcast(I32)
+        )
+        for quad in range(4):
+            nc.sync.dma_start(
+                out=w2_sc_raw[32 * quad : 32 * quad + 4, :].bitcast(I32).rearrange("r (a c) -> r a c", a=PASSES),
+                in_=w2_scales[:, 4 * quad : 4 * quad + 4, :].bitcast(I32).rearrange("a r c -> r a c"),
+            )
         load_table(0, placed([P, T], U32, "tab0", 0))
         w2_raw = sb([P, PASSES * 2 * H], U8, "w2_raw")
         nc.sync.dma_start(
@@ -106,47 +98,44 @@ def tile_list_proverb_kinship_scores_kernel(
         nc.sync.dma_start(pos2_sb[:], pos2)
         nc.sync.dma_start(pos1_sb[:], pos1)
 
-        w2_codes = sb([P, PASSES * 2 * H], U8, "w2_codes")
-        nc.vector.tensor_copy(
-            out=w2_codes[:].bitcast(I32).rearrange("p (a t q u) -> p a t q u", a=PASSES, t=PACK, u=2),
-            in_=w2_raw[:].bitcast(I32).rearrange("p (a q t u) -> p a t q u", a=PASSES, t=PACK, u=2),
-        )
-
+        v_sc = sb([P, S], U8, "v_sc")
+        nc.vector.tensor_copy(out=v_sc[:], in_=tab_sc[:].indirect(offs_sb[:]))
+        for a, queue in enumerate((nc.scalar, nc.gpsimd)):
+            for r in range(4):
+                queue.dma_start(
+                    out=planes[a][r:P:32, :].bitcast(I32), in_=v_sc[16 * a + r : 16 * (a + 1) : 4, :].bitcast(I32)
+                )
 
         cols = BANK // LIST_ROWS
         v = {}
         v0 = sb([P, S], U32, "v0")
         nc.vector.tensor_copy(out=v0[:], in_=tab[0][:].indirect(offs_sb[:]))
-        load_weight("w3", w3, 0, placed([P, PACK, H], F32, "w3_raw0", 2 * T))
-        v_sc = placed([P, S], U8, "v_sc", 0)
-        nc.vector.tensor_copy(out=v_sc[:], in_=tab_sc[:].indirect(offs_sb[:]))
-        nc.scalar.dma_start(out=v_sc1[0:100, :].bitcast(I32), in_=v_sc[4:104, :].bitcast(I32))
-        packed_planes = [v_sc[:], v_sc[4:P, :]]
-        level_planes = [v_sc[:], v_sc1[:]]
-        load_weight("w3", w3, 1, placed([P, PACK, H], F32, "w3_raw1", W3_AT))
+        for a in range(PASSES):
+            load_weight("w3", w3, a, placed([P, PACK, H], F32, f"w3_raw{a}", a * W3_LATE_AT))
 
-        w2_sc = sb([P, PASSES * H], U8, "w2_sc")
+        w2_sc = placed([P, PASSES * H], U8, "w2_sc", W2_SC_AT)
         nc.vector.tensor_copy(
             out=w2_sc[:].bitcast(I32).rearrange("p (a t q) -> p a t q", a=PASSES, t=PACK),
             in_=w2_sc_raw[:].bitcast(I32).rearrange("p (a q t) -> p a t q", a=PASSES, t=PACK),
         )
 
+        w2_codes = placed([P, PASSES * 2 * H], U8, "w2_codes", W2_CODES_AT)
+        nc.vector.tensor_copy(
+            out=w2_codes[:].bitcast(I32).rearrange("p (a t q u) -> p a t q u", a=PASSES, t=PACK, u=2),
+            in_=w2_raw[:].bitcast(I32).rearrange("p (a q t u) -> p a t q u", a=PASSES, t=PACK, u=2),
+        )
+
         for half in range(HALVES):
             v[0, half] = v0[:, half * BANK : (half + 1) * BANK]
         for half in range(HALVES):
-            v1 = placed([P, BANK], U32, f"v1_{half}", TAB_SC_AT + 1024 + 2048 * half)
+            v1 = sb([P, BANK], U32, f"v1_{half}")
             nc.vector.tensor_copy(
                 out=v1[:], in_=tab[1][:].indirect(offs_sb[:, half * cols : (half + 1) * cols])
             )
             v[1, half] = v1[:]
         load_weight("w1", w1, 0, placed([P, PACK, H], F32, "w1_raw0", TAB1_AT))
 
-        turned = bank("turned")
-        nc.tensor.transpose(turned[:, 0:P], rows[:], ident[:])
-        per_row = sb([P, PACK + BLOCKS], F32, "per_row")
-        nc.scalar.activation(out=per_row[:], in_=turned[:, 0 : PACK + BLOCKS], func=ACT.Copy)
-
-        def first_stage(name, operands, planes, t, half, order):
+        def first_stage(name, operands, t, half, order):
             acc = bank(f"{name}_{t}_{half}")
             for a in order:
                 codes, scales = operands[a, t]
@@ -175,15 +164,18 @@ def tile_list_proverb_kinship_scores_kernel(
             )
             return grouped
 
-        def quantise(name, grouped, tag=None):
+        def quantise(name, grouped, tag=None, offset=None):
             width = grouped.shape[1] // PACK
-            codes = sb([P, width], U32, f"{name}_codes", tag=tag)
+            if offset is None:
+                codes = sb([P, width], U32, f"{name}_codes", tag=tag)
+            else:
+                codes = placed([P, width], U32, f"{name}_codes", offset)
             scales = sb([P, width], U8, f"{name}_scales")
             nc.vector.quantize_mx(out=codes[:].bitcast(FP8X4), scales=scales[:], in_=grouped[:])
             return codes, scales
 
-        def quantise_weight(name, a, slots, grouped, operands, tag=None):
-            codes, scales = quantise(f"{name}_{a}_{slots[0]}", grouped, tag)
+        def quantise_weight(name, a, slots, grouped, operands, tag=None, offset=None):
+            codes, scales = quantise(f"{name}_{a}_{slots[0]}", grouped, tag, offset)
             for i, t in enumerate(slots):
                 operands[a, t] = (
                     codes[:, i * P : (i + 1) * P].bitcast(FP8X4),
@@ -199,40 +191,59 @@ def tile_list_proverb_kinship_scores_kernel(
         bent = {}
         for half in range(HALVES):
             for t in range(PACK):
-                acc = first_stage("tone", w2_ops, level_planes, t, half, [0, 1])
+                acc = first_stage("tone", w2_ops, t, half, [0, 1])
                 bent[t, half] = sb([P, BANK], F32, f"bent_{t}_{half}")
                 nc.scalar.activation(out=bent[t, half][:], in_=acc[:], func=ACT.Tanh)
 
         w3_ops = {}
         every = [0, 1, 2, 3]
         grouped = cast("w3", 0, every, nc.vector.tensor_copy, offset=TAB1_AT + 2 * T)
-        load_weight("w1", w1, 1, placed([P, PACK, H], F32, "w1_raw1", 2 * T))
+        load_weight("w1", w1, 1, placed([P, PACK, H], F32, "w1_raw1", 0))
         quantise_weight("w3", 0, every, grouped, w3_ops)
-        pairs = [([0, 1], nc.vector.tensor_copy, None), ([2, 3], nc.vector.tensor_copy, None)]
-        for slots, copy, tag in pairs:
-            quantise_weight("w3", 1, slots, cast("w3", 1, slots, copy, tag), w3_ops)
-            for t in slots:
-                for half in range(HALVES):
-                    acc = first_stage("image", w3_ops, packed_planes, t, half, [1, 0])
-                    if (t, half) == (PACK - 1, HALVES - 1):
-                        u[t, half] = placed([P, BANK], F32, f"u_{t}_{half}", PICK1_AT + 1024)
-                    else:
-                        u[t, half] = sb([P, BANK], F32, f"u_{t}_{half}")
-                    nc.vector.tensor_tensor(out=u[t, half][:], in0=acc[:], in1=bent[t, half][:], op=ALU.add)
+        for slots in ([0, 1], [2, 3]):
+            quantise_weight("w3", 1, slots, cast("w3", 1, slots, nc.vector.tensor_copy), w3_ops)
+        for half in range(HALVES):
+            for t in range(PACK):
+                acc = first_stage("image", w3_ops, t, half, [1, 0])
+                if (t, half) == (PACK - 1, HALVES - 1):
+                    u[t, half] = placed([P, BANK], F32, f"u_{t}_{half}", PICK1_AT + 1024)
+                else:
+                    u[t, half] = sb([P, BANK], F32, f"u_{t}_{half}")
+                nc.vector.tensor_tensor(out=u[t, half][:], in0=acc[:], in1=bent[t, half][:], op=ALU.add)
+
+        gain_sb = placed([P, PACK], F32, "gain_sb", TAB1_AT - 128)
+        cap_sb = placed([P, BLOCKS], F32, "cap_sb", TAB1_AT - 64)
+        with nc.allow_non_contiguous_dma(reason="one value a partition and slot"):
+            for e in range(4):
+                nc.sync.dma_start(out=gain_sb[e:P:4, :], in_=gain.rearrange("(q t e) -> e q t", t=PACK, e=4)[e])
+            nc.sync.dma_start(out=cap_sb[:], in_=cap.rearrange("(b p) -> p b", p=P))
+
+        sign_sb = sb([P, PACK], F32, "sign_sb")
+        nc.gpsimd.tensor_scalar(
+            out=sign_sb[:], in0=gain_sb[:], scalar1=0.0, scalar2=2.0, op0=ALU.is_ge, op1=ALU.mult
+        )
+        nc.gpsimd.tensor_scalar(
+            out=sign_sb[:], in0=sign_sb[:], scalar1=-1.0, scalar2=1.0, op0=ALU.add, op1=ALU.mult
+        )
 
         w1_ops = {}
-        quantise_weight("w1", 0, every, cast("w1", 0, every, nc.scalar.copy, "w2_codes"), w1_ops)
+        quantise_weight("w1", 0, every, cast("w1", 0, every, nc.scalar.copy, offset=W2_CODES_AT), w1_ops, tag="bent_3_0")
         w1_last = [cast("w1", 1, [t], nc.scalar.copy) for t in range(PACK)]
-        quantise_weight("w1", 1, [0], w1_last[0], w1_ops)
-        quantise_weight("w1", 1, [1], w1_last[1], w1_ops)
+        quantise_weight("w1", 1, [0], w1_last[0], w1_ops, tag="bent_1_1")
+        quantise_weight("w1", 1, [1], w1_last[1], w1_ops, tag="bent_3_1")
         h = []
         x2_bf = sb([P, PICK * PACK], BF16, "x2_bf")
         for t in range(PACK):
             h.append(sb([P, S], F32, f"h{t}"))
             for half in range(HALVES):
-                acc = first_stage("theme", w1_ops, packed_planes, t, half, [1, 0])
-                nc.vector.tensor_tensor(
-                    out=h[t][:, half * BANK : (half + 1) * BANK], in0=acc[:], in1=u[t, half][:], op=ALU.mult
+                acc = first_stage("theme", w1_ops, t, half, [1, 0])
+                nc.vector.scalar_tensor_tensor(
+                    out=h[t][:, half * BANK : (half + 1) * BANK],
+                    in0=acc[:],
+                    scalar=sign_sb[:, t : t + 1],
+                    in1=u[t, half][:],
+                    op0=ALU.mult,
+                    op1=ALU.mult,
                 )
             if t + 2 < PACK:
                 quantise_weight("w1", 1, [t + 2], w1_last[t + 2], w1_ops, tag=f"u_{t}_0")
@@ -241,32 +252,33 @@ def tile_list_proverb_kinship_scores_kernel(
             else:
                 picked2 = sb([P, PICK], F32, f"picked2_{t}")
             nc.vector.tensor_copy(out=picked2[:], in_=h[t][:].indirect(pos2_sb[:]))
-            nc.scalar.activation(out=picked2[:], in_=picked2[:], func=ACT.Abs)
             nc.scalar.activation(
                 out=x2_bf[:].rearrange("p (j t) -> p t j", t=PACK)[:, t, :],
                 in_=picked2[:],
-                func=ACT.Copy,
-                scale=per_row[:, t : t + 1],
+                func=ACT.Abs,
+                scale=gain_sb[:, t : t + 1],
             )
 
         cols1 = P // LIST_ROWS
         x1_bf = {}
         scores = {}
 
-        def pick1(b):
-            picked1 = placed([P, PACK, P], F32, f"picked1_{b}", PICK1_AT + 2048 * (b % 2))
+        def pick1(b0, n):
+            picked1 = placed([P, PACK, n * P], F32, f"picked1_{b0}", PICK1_AT + 2048 * (b0 % 2))
             for t in range(PACK):
                 nc.vector.tensor_copy(
-                    out=picked1[:, t, :], in_=h[t][:].indirect(pos1_sb[:, b * cols1 : (b + 1) * cols1])
+                    out=picked1[:, t, :], in_=h[t][:].indirect(pos1_sb[:, b0 * cols1 : (b0 + n) * cols1])
                 )
-            if b < 2:
-                x1_bf[b] = placed([P, P * PACK], BF16, f"x1_bf{b}", PICK2_AT + 1024 * b)
-            else:
-                x1_bf[b] = sb([P, P * PACK], BF16, f"x1_bf{b}")
-            nc.scalar.copy(
-                out=x1_bf[b][:].rearrange("p (c i t) -> p c t i", i=4, t=PACK),
-                in_=picked1[:].rearrange("p t (c i) -> p c t i", i=4),
-            )
+            for i in range(n):
+                b = b0 + i
+                if b < 2:
+                    x1_bf[b] = placed([P, P * PACK], BF16, f"x1_bf{b}", PICK2_AT + 1024 * b)
+                else:
+                    x1_bf[b] = sb([P, P * PACK], BF16, f"x1_bf{b}")
+                nc.scalar.copy(
+                    out=x1_bf[b][:].rearrange("p (c i t) -> p c t i", i=4, t=PACK),
+                    in_=picked1[:, :, i * P : (i + 1) * P].rearrange("p t (c i) -> p c t i", i=4),
+                )
 
         def score(b):
             x1_codes, x1_scales = quantise(f"x1_{b}", x1_bf[b])
@@ -281,25 +293,26 @@ def tile_list_proverb_kinship_scores_kernel(
                 stop=True,
             )
 
-        def finish(b):
-            capped = sb([P, PICK], F32, f"capped{b}")
-            nc.vector.tensor_scalar(
-                out=capped[:],
-                in0=scores[b][:],
-                scalar1=per_row[:, PACK + b : PACK + b + 1],
-                scalar2=None,
-                op0=ALU.min,
-            )
-            nc.scalar.activation(out=capped[:], in_=capped[:], func=ACT.Exp)
-            nc.sync.dma_start(out=out[b * P : (b + 1) * P, :], in_=capped[:])
+        def finish(b, pieces):
+            width = PICK // pieces
+            for i in range(pieces):
+                span = slice(i * width, (i + 1) * width)
+                capped = sb([P, width], F32, f"capped{b}_{i}")
+                nc.vector.tensor_scalar(
+                    out=capped[:], in0=scores[b][:, span], scalar1=cap_sb[:, b : b + 1], scalar2=None, op0=ALU.min
+                )
+                nc.scalar.activation(out=capped[:], in_=capped[:], func=ACT.Exp)
+                nc.sync.dma_start(out=out[b * P : (b + 1) * P, span], in_=capped[:])
 
-        pick1(0)
-        pick1(1)
+        pick1(0, 2)
         x2_codes, x2_scales = quantise("x2", x2_bf)
-        for b in range(BLOCKS + 1):
-            if b < BLOCKS:
-                score(b)
-            if b >= 1:
-                finish(b - 1)
-            if b + 2 < BLOCKS:
-                pick1(b + 2)
+        score(0)
+        pick1(2, 1)
+        pick1(3, 1)
+        score(1)
+        finish(0, 1)
+        score(2)
+        score(3)
+        finish(1, 1)
+        finish(2, 1)
+        finish(3, 2)

@@ -205,8 +205,10 @@ def tile_list_proverb_kinship_scores_kernel(
         for half in range(HALVES):
             for t in range(PACK):
                 acc = first_stage("image", w3_ops, t, half, [1, 0])
-                if (t, half) == (PACK - 1, HALVES - 1):
-                    u[t, half] = placed([P, BANK], F32, f"u_{t}_{half}", PICK1_AT + 1024)
+                if (t, half) == (PACK - 2, HALVES - 1):
+                    u[t, half] = placed([P, BANK], F32, f"u_{t}_{half}", PICK1_AT)
+                elif (t, half) == (PACK - 2, 0):
+                    u[t, half] = placed([P, BANK], F32, f"u_{t}_{half}", PICK2_AT + 2048)
                 else:
                     u[t, half] = sb([P, BANK], F32, f"u_{t}_{half}")
                 nc.vector.tensor_tensor(out=u[t, half][:], in0=acc[:], in1=bent[t, half][:], op=ALU.add)
@@ -228,13 +230,13 @@ def tile_list_proverb_kinship_scores_kernel(
 
         w1_ops = {}
         quantise_weight("w1", 0, every, cast("w1", 0, every, nc.scalar.copy, offset=W2_CODES_AT), w1_ops, tag="bent_3_0")
-        w1_last = [cast("w1", 1, [t], nc.scalar.copy) for t in range(PACK)]
+        w1_last = {t: cast("w1", 1, [t], nc.scalar.copy) for t in (0, 1, 3, 2)}
         quantise_weight("w1", 1, [0], w1_last[0], w1_ops, tag="bent_1_1")
         quantise_weight("w1", 1, [1], w1_last[1], w1_ops, tag="bent_3_1")
-        h = []
+        h = [sb([P, S], F32, f"h{t}") for t in range(PACK)]
         x2_bf = sb([P, PICK * PACK], BF16, "x2_bf")
-        for t in range(PACK):
-            h.append(sb([P, S], F32, f"h{t}"))
+
+        def product(t):
             for half in range(HALVES):
                 acc = first_stage("theme", w1_ops, t, half, [1, 0])
                 nc.vector.scalar_tensor_tensor(
@@ -245,10 +247,22 @@ def tile_list_proverb_kinship_scores_kernel(
                     op0=ALU.mult,
                     op1=ALU.mult,
                 )
-            if t + 2 < PACK:
-                quantise_weight("w1", 1, [t + 2], w1_last[t + 2], w1_ops, tag=f"u_{t}_0")
-            if t == PACK - 1:
-                picked2 = placed([P, PICK], F32, f"picked2_{t}", PICK2_AT)
+
+        def product_beside(t):
+            for half in range(HALVES):
+                acc = first_stage("theme", w1_ops, t, half, [1, 0])
+                if half == HALVES - 1:
+                    theme = placed([P, BANK], F32, f"theme_{half}", PICK1_AT + 2048)
+                else:
+                    theme = sb([P, BANK], F32, f"theme_{half}")
+                nc.scalar.activation(out=theme[:], in_=acc[:], func=ACT.Copy, scale=sign_sb[:, t : t + 1])
+                nc.gpsimd.tensor_tensor(
+                    out=h[t][:, half * BANK : (half + 1) * BANK], in0=theme[:], in1=u[t, half][:], op=ALU.mult
+                )
+
+        def pick2(t):
+            if t >= 2:
+                picked2 = placed([P, PICK], F32, f"picked2_{t}", PICK2_AT + 2048 * (t - 2))
             else:
                 picked2 = sb([P, PICK], F32, f"picked2_{t}")
             nc.vector.tensor_copy(out=picked2[:], in_=h[t][:].indirect(pos2_sb[:]))
@@ -259,24 +273,35 @@ def tile_list_proverb_kinship_scores_kernel(
                 scale=gain_sb[:, t : t + 1],
             )
 
+        product(0)
+        quantise_weight("w1", 1, [3], w1_last[3], w1_ops, tag="u_0_0")
+        quantise_weight("w1", 1, [2], w1_last[2], w1_ops, tag="u_0_1")
+        product_beside(3)
+        pick2(0)
+        product(1)
+        pick2(1)
+        product(2)
+        pick2(2)
+        pick2(3)
+
         cols1 = P // LIST_ROWS
         x1_bf = {}
         scores = {}
 
         def pick1(b0, n):
-            picked1 = placed([P, PACK, n * P], F32, f"picked1_{b0}", PICK1_AT + 2048 * (b0 % 2))
+            picked1 = placed([P, PACK, n * P], F32, f"picked1_{b0}", PICK1_AT)
             for t in range(PACK):
                 nc.vector.tensor_copy(
                     out=picked1[:, t, :], in_=h[t][:].indirect(pos1_sb[:, b0 * cols1 : (b0 + n) * cols1])
                 )
+            if b0 == 0:
+                grouped = placed([P, n * P * PACK], BF16, f"x1_bf{b0}", PICK2_AT + 1024)
+            else:
+                grouped = sb([P, n * P * PACK], BF16, f"x1_bf{b0}")
             for i in range(n):
-                b = b0 + i
-                if b < 2:
-                    x1_bf[b] = placed([P, P * PACK], BF16, f"x1_bf{b}", PICK2_AT + 1024 * b)
-                else:
-                    x1_bf[b] = sb([P, P * PACK], BF16, f"x1_bf{b}")
+                x1_bf[b0 + i] = grouped[:, i * P * PACK : (i + 1) * P * PACK]
                 nc.scalar.copy(
-                    out=x1_bf[b][:].rearrange("p (c i t) -> p c t i", i=4, t=PACK),
+                    out=x1_bf[b0 + i].rearrange("p (c i t) -> p c t i", i=4, t=PACK),
                     in_=picked1[:, :, i * P : (i + 1) * P].rearrange("p t (c i) -> p c t i", i=4),
                 )
 
@@ -302,17 +327,17 @@ def tile_list_proverb_kinship_scores_kernel(
                     out=capped[:], in0=scores[b][:, span], scalar1=cap_sb[:, b : b + 1], scalar2=None, op0=ALU.min
                 )
                 nc.scalar.activation(out=capped[:], in_=capped[:], func=ACT.Exp)
-                nc.sync.dma_start(out=out[b * P : (b + 1) * P, span], in_=capped[:])
+                queue = nc.scalar if i == 1 else nc.sync
+                queue.dma_start(out=out[b * P : (b + 1) * P, span], in_=capped[:])
 
         pick1(0, 2)
         x2_codes, x2_scales = quantise("x2", x2_bf)
         score(0)
-        pick1(2, 1)
-        pick1(3, 1)
         score(1)
+        pick1(2, 2)
         finish(0, 1)
+        finish(1, 1)
         score(2)
         score(3)
-        finish(1, 1)
         finish(2, 1)
         finish(3, 2)

@@ -18,17 +18,28 @@ ALU = mybir.AluOpType
 
 P = 128
 PACK = 4
+RUN = 4
 PASSES = K // (P * PACK)
+QUADS = 4
+QUAD = P // QUADS
+QUAD_ROWS = 4
+PASS_ROWS = QUADS * QUAD_ROWS
 BANK = 512
+PSUM_BANKS = 8
 HALVES = S // BANK
 BLOCKS = PICK // P
 LIST_ROWS = 16
-W2_SC_AT = 8192
-W2_CODES_AT = 9216
-W3_LATE_AT = 11264
-TAB1_AT = W3_LATE_AT + 8192
-PICK1_AT = TAB1_AT + 4 * T
-PICK2_AT = PICK1_AT + 4096
+
+RAW_BYTES = PACK * H * 4
+TAB0_AT = 0
+EARLY_RAW_AT = TAB0_AT
+W2_SC_AT = EARLY_RAW_AT + RAW_BYTES
+W2_CODES_AT = W2_SC_AT + PASSES * H
+LATE_RAW_AT = W2_CODES_AT + PASSES * 2 * H
+TAB1_AT = LATE_RAW_AT + RAW_BYTES
+PICK2_AT = TAB1_AT + 4 * T
+LAST_TANH_AT = PICK2_AT + 4 * BANK
+X2_AT = LAST_TANH_AT + 4 * BANK
 
 
 def tile_list_proverb_kinship_scores_kernel(
@@ -38,13 +49,12 @@ def tile_list_proverb_kinship_scores_kernel(
     with ExitStack() as ctx:
         keep = ctx.enter_context(tc.tile_pool(name="keep", bufs=1))
         shared = ctx.enter_context(tc.tile_pool(name="shared", bufs=1))
-        psum = ctx.enter_context(tc.psum_pool(name="psum", bufs=8))
+        psum = ctx.enter_context(tc.psum_pool(name="psum", bufs=PSUM_BANKS))
 
-        def sb(shape, dtype, name, tag=None):
-            return keep.tile(shape, dtype, name=name, tag=tag or name, align_bytes=64)
-
-        def placed(shape, dtype, name, offset):
-            return shared.tile(shape, dtype, name=name, align_bytes=64, offset=offset)
+        def sb(shape, dtype, name, over=None):
+            if isinstance(over, int):
+                return shared.tile(shape, dtype, name=name, align_bytes=64, offset=over)
+            return keep.tile(shape, dtype, name=name, tag=over or name, align_bytes=64)
 
         def bank(name):
             return psum.tile([P, BANK], F32, name=name, tag="bank")
@@ -54,10 +64,17 @@ def tile_list_proverb_kinship_scores_kernel(
         pos2_sb = sb([P, PICK // LIST_ROWS], U16, "pos2_sb")
 
         tab_sc = sb([P, T], U8, "tab_sc")
-        nc.vector.memset(tab_sc[32:64, :].bitcast(I32), 0)
-        nc.vector.memset(tab_sc[64:P, :].bitcast(I32), 0)
+        nc.vector.memset(tab_sc[QUAD : 2 * QUAD, :].bitcast(I32), 0)
+        nc.vector.memset(tab_sc[2 * QUAD : P, :].bitcast(I32), 0)
         w2_sc_raw = sb([P, PASSES * H], U8, "w2_sc_raw")
         nc.gpsimd.memset(w2_sc_raw[:].bitcast(I32), 0)
+        for quad in range(QUADS):
+            nc.gpsimd.dma_start(
+                out=w2_sc_raw[QUAD * quad : QUAD * quad + QUAD_ROWS, :]
+                .bitcast(I32)
+                .rearrange("i (a c) -> i a c", a=PASSES),
+                in_=w2_scales[:, QUAD_ROWS * quad : QUAD_ROWS * (quad + 1), :].bitcast(I32).rearrange("a i c -> i a c"),
+            )
         planes = []
         for a in range(PASSES):
             planes.append(sb([P, S], U8, f"plane{a}"))
@@ -66,14 +83,14 @@ def tile_list_proverb_kinship_scores_kernel(
         tab = {}
         raw = {}
 
-        def load_table(a, tile):
-            tab[a] = tile
+        def load_table(a, at):
+            tab[a] = sb([P, T], U32, f"tab{a}", at)
             nc.sync.dma_start(
                 out=tab[a][:].bitcast(I32), in_=tab_words[a].rearrange("p t i -> p (t i)").bitcast(I32)
             )
 
-        def load_weight(name, w, a, tile):
-            raw[name, a] = tile
+        def load_weight(name, w, a, at):
+            raw[name, a] = sb([P, PACK, H], F32, f"{name}_raw{a}", at)
             nc.sync.dma_start(
                 out=raw[name, a][:],
                 in_=w[a * P * PACK : (a + 1) * P * PACK, :].rearrange("(p j) r -> p j r", j=PACK),
@@ -81,59 +98,54 @@ def tile_list_proverb_kinship_scores_kernel(
 
         nc.sync.dma_start(offs_sb[:], offs)
         nc.sync.dma_start(
-            out=tab_sc[0:32, :].bitcast(I32), in_=tab_scales.rearrange("a q t -> (a q) t").bitcast(I32)
+            out=tab_sc[0 : PASSES * PASS_ROWS, :].bitcast(I32),
+            in_=tab_scales.rearrange("a q t -> (a q) t").bitcast(I32),
         )
-        for quad in range(4):
-            nc.sync.dma_start(
-                out=w2_sc_raw[32 * quad : 32 * quad + 4, :].bitcast(I32).rearrange("r (a c) -> r a c", a=PASSES),
-                in_=w2_scales[:, 4 * quad : 4 * quad + 4, :].bitcast(I32).rearrange("a r c -> r a c"),
-            )
-        load_table(0, placed([P, T], U32, "tab0", 0))
+        load_table(0, TAB0_AT)
         w2_raw = sb([P, PASSES * 2 * H], U8, "w2_raw")
         nc.sync.dma_start(
             out=w2_raw[:].bitcast(I32).rearrange("p (a c) -> p a c", a=PASSES),
             in_=w2_words.bitcast(I32).rearrange("a p c -> p a c"),
         )
-        load_table(1, placed([P, T], U32, "tab1", TAB1_AT))
+        load_table(1, TAB1_AT)
         nc.sync.dma_start(pos2_sb[:], pos2)
         nc.sync.dma_start(pos1_sb[:], pos1)
 
         v_sc = sb([P, S], U8, "v_sc")
         nc.vector.tensor_copy(out=v_sc[:], in_=tab_sc[:].indirect(offs_sb[:]))
         for a, queue in enumerate((nc.scalar, nc.gpsimd)):
-            for r in range(4):
+            for i in range(QUAD_ROWS):
                 queue.dma_start(
-                    out=planes[a][r:P:32, :].bitcast(I32), in_=v_sc[16 * a + r : 16 * (a + 1) : 4, :].bitcast(I32)
+                    out=planes[a][i:P:QUAD, :].bitcast(I32),
+                    in_=v_sc[PASS_ROWS * a + i : PASS_ROWS * (a + 1) : QUAD_ROWS, :].bitcast(I32),
                 )
 
-        cols = BANK // LIST_ROWS
         v = {}
         v0 = sb([P, S], U32, "v0")
         nc.vector.tensor_copy(out=v0[:], in_=tab[0][:].indirect(offs_sb[:]))
-        for a in range(PASSES):
-            load_weight("w3", w3, a, placed([P, PACK, H], F32, f"w3_raw{a}", a * W3_LATE_AT))
+        load_weight("w3", w3, 0, EARLY_RAW_AT)
+        load_weight("w3", w3, 1, LATE_RAW_AT)
 
-        w2_sc = placed([P, PASSES * H], U8, "w2_sc", W2_SC_AT)
+        w2_sc = sb([P, PASSES * H], U8, "w2_sc", W2_SC_AT)
         nc.vector.tensor_copy(
             out=w2_sc[:].bitcast(I32).rearrange("p (a t q) -> p a t q", a=PASSES, t=PACK),
             in_=w2_sc_raw[:].bitcast(I32).rearrange("p (a q t) -> p a t q", a=PASSES, t=PACK),
         )
-
-        w2_codes = placed([P, PASSES * 2 * H], U8, "w2_codes", W2_CODES_AT)
+        w2_codes = sb([P, PASSES * 2 * H], U8, "w2_codes", W2_CODES_AT)
         nc.vector.tensor_copy(
-            out=w2_codes[:].bitcast(I32).rearrange("p (a t q u) -> p a t q u", a=PASSES, t=PACK, u=2),
-            in_=w2_raw[:].bitcast(I32).rearrange("p (a q t u) -> p a t q u", a=PASSES, t=PACK, u=2),
+            out=w2_codes[:].bitcast(I32).rearrange("p (a t q two) -> p a t q two", a=PASSES, t=PACK, two=2),
+            in_=w2_raw[:].bitcast(I32).rearrange("p (a q t two) -> p a t q two", a=PASSES, t=PACK, two=2),
         )
 
+        half_cols = BANK // LIST_ROWS
         for half in range(HALVES):
             v[0, half] = v0[:, half * BANK : (half + 1) * BANK]
-        for half in range(HALVES):
             v1 = sb([P, BANK], U32, f"v1_{half}")
             nc.vector.tensor_copy(
-                out=v1[:], in_=tab[1][:].indirect(offs_sb[:, half * cols : (half + 1) * cols])
+                out=v1[:], in_=tab[1][:].indirect(offs_sb[:, half * half_cols : (half + 1) * half_cols])
             )
             v[1, half] = v1[:]
-        load_weight("w1", w1, 0, placed([P, PACK, H], F32, "w1_raw0", TAB1_AT))
+        load_weight("w1", w1, 0, TAB1_AT)
 
         def first_stage(name, operands, t, half, order):
             acc = bank(f"{name}_{t}_{half}")
@@ -150,32 +162,26 @@ def tile_list_proverb_kinship_scores_kernel(
                 )
             return acc
 
-        def cast(name, a, slots, copy, tag=None, offset=None):
+        def round_weight(name, a, slots, copy, over=None):
             n = len(slots)
-            if offset is None:
-                grouped = sb([P, n * P * PACK], BF16, f"{name}_bf{a}_{slots[0]}", tag=tag)
-            else:
-                grouped = placed([P, n * P * PACK], BF16, f"{name}_bf{a}_{slots[0]}", offset)
+            grouped = sb([P, n * P * PACK], BF16, f"{name}_bf{a}_{slots[0]}", over)
             copy(
-                out=grouped[:].rearrange("p (t q e j) -> p t q j e", t=n, e=4, j=PACK),
-                in_=raw[name, a][:].rearrange("p j (q t e) -> p t q j e", t=PACK, e=4)[
+                out=grouped[:].rearrange("p (t q e j) -> p t q j e", t=n, e=RUN, j=PACK),
+                in_=raw[name, a][:].rearrange("p j (q t e) -> p t q j e", t=PACK, e=RUN)[
                     :, slots[0] : slots[0] + n
                 ],
             )
             return grouped
 
-        def quantise(name, grouped, tag=None, offset=None):
+        def quantise(name, grouped, over=None):
             width = grouped.shape[1] // PACK
-            if offset is None:
-                codes = sb([P, width], U32, f"{name}_codes", tag=tag)
-            else:
-                codes = placed([P, width], U32, f"{name}_codes", offset)
+            codes = sb([P, width], U32, f"{name}_codes", over)
             scales = sb([P, width], U8, f"{name}_scales")
             nc.vector.quantize_mx(out=codes[:].bitcast(FP8X4), scales=scales[:], in_=grouped[:])
             return codes, scales
 
-        def quantise_weight(name, a, slots, grouped, operands, tag=None, offset=None):
-            codes, scales = quantise(f"{name}_{a}_{slots[0]}", grouped, tag, offset)
+        def quantise_weight(name, a, slots, grouped, operands, over=None):
+            codes, scales = quantise(f"{name}_{a}_{slots[0]}", grouped, over)
             for i, t in enumerate(slots):
                 operands[a, t] = (
                     codes[:, i * P : (i + 1) * P].bitcast(FP8X4),
@@ -187,37 +193,35 @@ def tile_list_proverb_kinship_scores_kernel(
             for t in range(PACK):
                 c0 = a * H + t * P
                 w2_ops[a, t] = (w2_codes[:, 2 * c0 : 2 * (c0 + P)].bitcast(FP4X4), w2_sc[:, c0 : c0 + P])
-        u = {}
-        bent = {}
+        tanh = {}
+        tanh_over = {(PACK - 1, HALVES - 1): LAST_TANH_AT}
         for half in range(HALVES):
             for t in range(PACK):
                 acc = first_stage("tone", w2_ops, t, half, [0, 1])
-                bent[t, half] = sb([P, BANK], F32, f"bent_{t}_{half}")
-                nc.scalar.activation(out=bent[t, half][:], in_=acc[:], func=ACT.Tanh)
+                tanh[t, half] = sb([P, BANK], F32, f"tanh_{t}_{half}", tanh_over.get((t, half)))
+                nc.scalar.activation(out=tanh[t, half][:], in_=acc[:], func=ACT.Tanh)
 
+        late_first = [1, 0]
+        every = list(range(PACK))
         w3_ops = {}
-        every = [0, 1, 2, 3]
-        grouped = cast("w3", 0, every, nc.vector.tensor_copy, offset=TAB1_AT + 2 * T)
-        load_weight("w1", w1, 1, placed([P, PACK, H], F32, "w1_raw1", 0))
-        quantise_weight("w3", 0, every, grouped, w3_ops)
-        for slots in ([0, 1], [2, 3]):
-            quantise_weight("w3", 1, slots, cast("w3", 1, slots, nc.vector.tensor_copy), w3_ops)
+        w3_early = round_weight("w3", 0, every, nc.vector.tensor_copy, TAB1_AT + RAW_BYTES)
+        load_weight("w1", w1, 1, EARLY_RAW_AT)
+        quantise_weight("w3", 0, every, w3_early, w3_ops)
+        for slots in (every[:2], every[2:]):
+            quantise_weight("w3", 1, slots, round_weight("w3", 1, slots, nc.vector.tensor_copy), w3_ops)
+        u = {}
+        u_over = {(0, 0): X2_AT, (1, 0): PICK2_AT}
         for half in range(HALVES):
             for t in range(PACK):
-                acc = first_stage("image", w3_ops, t, half, [1, 0])
-                if (t, half) == (PACK - 2, HALVES - 1):
-                    u[t, half] = placed([P, BANK], F32, f"u_{t}_{half}", PICK1_AT)
-                elif (t, half) == (PACK - 2, 0):
-                    u[t, half] = placed([P, BANK], F32, f"u_{t}_{half}", PICK2_AT + 2048)
-                else:
-                    u[t, half] = sb([P, BANK], F32, f"u_{t}_{half}")
-                nc.vector.tensor_tensor(out=u[t, half][:], in0=acc[:], in1=bent[t, half][:], op=ALU.add)
+                acc = first_stage("image", w3_ops, t, half, late_first)
+                u[t, half] = sb([P, BANK], F32, f"u_{t}_{half}", u_over.get((t, half)))
+                nc.vector.tensor_tensor(out=u[t, half][:], in0=acc[:], in1=tanh[t, half][:], op=ALU.add)
 
-        gain_sb = placed([P, PACK], F32, "gain_sb", TAB1_AT - 128)
-        cap_sb = placed([P, BLOCKS], F32, "cap_sb", TAB1_AT - 64)
+        gain_sb = sb([P, PACK], F32, "gain_sb", TAB1_AT - 128)
+        cap_sb = sb([P, BLOCKS], F32, "cap_sb", TAB1_AT - 64)
         with nc.allow_non_contiguous_dma(reason="one value a partition and slot"):
-            for e in range(4):
-                nc.sync.dma_start(out=gain_sb[e:P:4, :], in_=gain.rearrange("(q t e) -> e q t", t=PACK, e=4)[e])
+            for e in range(RUN):
+                nc.sync.dma_start(out=gain_sb[e:P:RUN, :], in_=gain.rearrange("(q t e) -> e q t", t=PACK, e=RUN)[e])
             nc.sync.dma_start(out=cap_sb[:], in_=cap.rearrange("(b p) -> p b", p=P))
 
         sign_sb = sb([P, PACK], F32, "sign_sb")
@@ -229,16 +233,18 @@ def tile_list_proverb_kinship_scores_kernel(
         )
 
         w1_ops = {}
-        quantise_weight("w1", 0, every, cast("w1", 0, every, nc.scalar.copy, offset=W2_CODES_AT), w1_ops, tag="bent_3_0")
-        w1_last = {t: cast("w1", 1, [t], nc.scalar.copy) for t in (0, 1, 3, 2)}
-        quantise_weight("w1", 1, [0], w1_last[0], w1_ops, tag="bent_1_1")
-        quantise_weight("w1", 1, [1], w1_last[1], w1_ops, tag="bent_3_1")
-        h = [sb([P, S], F32, f"h{t}") for t in range(PACK)]
-        x2_bf = sb([P, PICK * PACK], BF16, "x2_bf")
+        w1_early = round_weight("w1", 0, every, nc.scalar.copy, W2_CODES_AT)
+        quantise_weight("w1", 0, every, w1_early, w1_ops, "tanh_1_1")
+        w1_late = {t: round_weight("w1", 1, [t], nc.scalar.copy) for t in (0, 1, 3, 2)}
+        quantise_weight("w1", 1, [0], w1_late[0], w1_ops, "tanh_2_1")
+        quantise_weight("w1", 1, [1], w1_late[1], w1_ops, LAST_TANH_AT)
+        quantise_weight("w1", 1, [3], w1_late[3], w1_ops, LAST_TANH_AT + 4 * P)
 
-        def product(t):
+        h = [sb([P, S], F32, f"h{t}") for t in range(PACK)]
+
+        def product_on_vector(t):
             for half in range(HALVES):
-                acc = first_stage("theme", w1_ops, t, half, [1, 0])
+                acc = first_stage("theme", w1_ops, t, half, late_first)
                 nc.vector.scalar_tensor_tensor(
                     out=h[t][:, half * BANK : (half + 1) * BANK],
                     in0=acc[:],
@@ -248,62 +254,64 @@ def tile_list_proverb_kinship_scores_kernel(
                     op1=ALU.mult,
                 )
 
-        def product_beside(t):
+        picked1 = sb([P, PACK, PICK], F32, "picked1")
+
+        def product_on_gpsimd(t, staging):
             for half in range(HALVES):
-                acc = first_stage("theme", w1_ops, t, half, [1, 0])
-                if half == HALVES - 1:
-                    theme = placed([P, BANK], F32, f"theme_{half}", PICK1_AT + 2048)
-                else:
-                    theme = sb([P, BANK], F32, f"theme_{half}")
-                nc.scalar.activation(out=theme[:], in_=acc[:], func=ACT.Copy, scale=sign_sb[:, t : t + 1])
+                acc = first_stage("theme", w1_ops, t, half, late_first)
+                nc.scalar.activation(out=staging[half], in_=acc[:], func=ACT.Copy, scale=sign_sb[:, t : t + 1])
                 nc.gpsimd.tensor_tensor(
-                    out=h[t][:, half * BANK : (half + 1) * BANK], in0=theme[:], in1=u[t, half][:], op=ALU.mult
+                    out=h[t][:, half * BANK : (half + 1) * BANK], in0=staging[half], in1=u[t, half][:], op=ALU.mult
                 )
 
-        def pick2(t):
-            if t >= 2:
-                picked2 = placed([P, PICK], F32, f"picked2_{t}", PICK2_AT + 2048 * (t - 2))
-            else:
-                picked2 = sb([P, PICK], F32, f"picked2_{t}")
+        def pick2(t, over=None):
+            picked2 = sb([P, PICK], F32, f"picked2_{t}", over)
             nc.vector.tensor_copy(out=picked2[:], in_=h[t][:].indirect(pos2_sb[:]))
             nc.scalar.activation(
-                out=x2_bf[:].rearrange("p (j t) -> p t j", t=PACK)[:, t, :],
+                out=x2_pairs[:].rearrange("p (pair j side) -> p pair side j", pair=2, side=2)[:, t // 2, t % 2, :],
                 in_=picked2[:],
                 func=ACT.Abs,
                 scale=gain_sb[:, t : t + 1],
             )
 
-        product(0)
-        quantise_weight("w1", 1, [3], w1_last[3], w1_ops, tag="u_0_0")
-        quantise_weight("w1", 1, [2], w1_last[2], w1_ops, tag="u_0_1")
-        product_beside(3)
-        pick2(0)
-        product(1)
-        pick2(1)
-        product(2)
-        pick2(2)
-        pick2(3)
-
-        cols1 = P // LIST_ROWS
-        x1_bf = {}
-        scores = {}
-
-        def pick1(b0, n):
-            picked1 = placed([P, PACK, n * P], F32, f"picked1_{b0}", PICK1_AT)
-            for t in range(PACK):
+        def pick1(t, pieces):
+            width = PICK // pieces
+            for i in range(pieces):
                 nc.vector.tensor_copy(
-                    out=picked1[:, t, :], in_=h[t][:].indirect(pos1_sb[:, b0 * cols1 : (b0 + n) * cols1])
+                    out=picked1[:, t, i * width : (i + 1) * width],
+                    in_=h[t][:].indirect(pos1_sb[:, i * width // LIST_ROWS : (i + 1) * width // LIST_ROWS]),
                 )
-            if b0 == 0:
-                grouped = placed([P, n * P * PACK], BF16, f"x1_bf{b0}", PICK2_AT + 1024)
-            else:
-                grouped = sb([P, n * P * PACK], BF16, f"x1_bf{b0}")
-            for i in range(n):
-                x1_bf[b0 + i] = grouped[:, i * P * PACK : (i + 1) * P * PACK]
-                nc.scalar.copy(
-                    out=x1_bf[b0 + i].rearrange("p (c i t) -> p c t i", i=4, t=PACK),
-                    in_=picked1[:, :, i * P : (i + 1) * P].rearrange("p t (c i) -> p c t i", i=4),
-                )
+
+        product_on_vector(0)
+        quantise_weight("w1", 1, [2], w1_late[2], w1_ops, X2_AT)
+        product_on_gpsimd(3, [sb([P, BANK], F32, "theme3")[:], picked1[:, 1, :]])
+        product_on_gpsimd(2, [sb([P, BANK], F32, "theme2")[:], picked1[:, 3, :]])
+        x2_pairs = sb([P, PICK * PACK], BF16, "x2_pairs", X2_AT)
+        pick2(0)
+        product_on_vector(1)
+        pick2(1)
+        pick1(0, 1)
+        pick2(3, PICK2_AT)
+        pick1(1, 1)
+        pick2(2)
+        x2_bf = sb([P, PICK * PACK], BF16, "x2_bf")
+        nc.scalar.copy(
+            out=x2_bf[:].bitcast(U32).rearrange("p (j pair) -> p j pair", pair=2),
+            in_=x2_pairs[:].bitcast(U32).rearrange("p (pair j) -> p j pair", pair=2),
+        )
+        pick1(3, 1)
+        pick1(2, BLOCKS)
+
+        x1_bf = []
+        for b in range(BLOCKS):
+            x1_bf.append(sb([P, P * PACK], BF16, f"x1_bf{b}"))
+            nc.scalar.copy(
+                out=x1_bf[b][:].rearrange("p (c i t) -> p c t i", i=RUN, t=PACK),
+                in_=picked1[:, :, b * P : (b + 1) * P].rearrange("p t (c i) -> p c t i", i=RUN),
+            )
+
+        x2_codes, x2_scales = quantise("x2", x2_bf)
+        scores = {}
 
         def score(b):
             x1_codes, x1_scales = quantise(f"x1_{b}", x1_bf[b])
@@ -318,26 +326,21 @@ def tile_list_proverb_kinship_scores_kernel(
                 stop=True,
             )
 
-        def finish(b, pieces):
-            width = PICK // pieces
-            for i in range(pieces):
+        def finish(b, queues):
+            width = PICK // len(queues)
+            for i, queue in enumerate(queues):
                 span = slice(i * width, (i + 1) * width)
                 capped = sb([P, width], F32, f"capped{b}_{i}")
                 nc.vector.tensor_scalar(
                     out=capped[:], in0=scores[b][:, span], scalar1=cap_sb[:, b : b + 1], scalar2=None, op0=ALU.min
                 )
                 nc.scalar.activation(out=capped[:], in_=capped[:], func=ACT.Exp)
-                queue = nc.scalar if i == 1 else nc.sync
                 queue.dma_start(out=out[b * P : (b + 1) * P, span], in_=capped[:])
 
-        pick1(0, 2)
-        x2_codes, x2_scales = quantise("x2", x2_bf)
-        score(0)
-        score(1)
-        pick1(2, 2)
-        finish(0, 1)
-        finish(1, 1)
-        score(2)
-        score(3)
-        finish(2, 1)
-        finish(3, 2)
+        for b in range(BLOCKS - 1):
+            score(b)
+        finish(0, [nc.sync])
+        score(BLOCKS - 1)
+        for b in range(1, BLOCKS - 1):
+            finish(b, [nc.sync])
+        finish(BLOCKS - 1, [nc.sync, nc.scalar])

from contextlib import ExitStack

import concourse.mybir as mybir

K, H, T, S, PICK = 1024, 512, 4096, 1024, 512
FLOPS = 2 * (3 * K * H * S + H * PICK * PICK)

F32 = mybir.dt.float32
BF16 = mybir.dt.bfloat16
I32 = mybir.dt.int32
U32 = mybir.dt.uint32
U16 = mybir.dt.uint16
U8 = mybir.dt.uint8
FP8X4 = mybir.dt.float8_e4m3fn_x4
FP4X4 = mybir.dt.float4_e2m1fn_x4
ACT = mybir.ActivationFunctionType
ALU = mybir.AluOpType

P = 128
PACK = 4
RUN = 4
PASSES = K // (P * PACK)
QUADS = 4
QUAD = P // QUADS
QUAD_ROWS = 4
PASS_ROWS = QUADS * QUAD_ROWS
BANK = 512
PSUM_BANKS = 8
HALVES = S // BANK
BLOCKS = PICK // P
LIST_ROWS = 16

RAW_BYTES = PACK * H * 4
TAB0_AT = 0
EARLY_RAW_AT = TAB0_AT
W2_SC_AT = EARLY_RAW_AT + RAW_BYTES
W2_CODES_AT = W2_SC_AT + PASSES * H
LATE_RAW_AT = W2_CODES_AT + PASSES * 2 * H
TAB1_AT = LATE_RAW_AT + RAW_BYTES
PICK2_AT = TAB1_AT + 4 * T
LAST_TANH_AT = PICK2_AT + 4 * BANK
X2_AT = LAST_TANH_AT + 4 * BANK


def tile_list_proverb_kinship_scores_kernel(
    tc, tab_words, tab_scales, offs, pos1, pos2, w1, w2_words, w2_scales, w3, gain, cap, out
):
    nc = tc.nc
    with ExitStack() as ctx:
        keep = ctx.enter_context(tc.tile_pool(name="keep", bufs=1))
        shared = ctx.enter_context(tc.tile_pool(name="shared", bufs=1))
        psum = ctx.enter_context(tc.psum_pool(name="psum", bufs=PSUM_BANKS))

        def sb(shape, dtype, name, over=None):
            if isinstance(over, int):
                return shared.tile(shape, dtype, name=name, align_bytes=64, offset=over)
            return keep.tile(shape, dtype, name=name, tag=over or name, align_bytes=64)

        def bank(name):
            return psum.tile([P, BANK], F32, name=name, tag="bank")

        offs_sb = sb([P, S // LIST_ROWS], U16, "offs_sb")
        pos1_sb = sb([P, PICK // LIST_ROWS], U16, "pos1_sb")
        pos2_sb = sb([P, PICK // LIST_ROWS], U16, "pos2_sb")

        tab_sc = sb([P, T], U8, "tab_sc")
        nc.vector.memset(tab_sc[QUAD : 2 * QUAD, :].bitcast(I32), 0)
        nc.vector.memset(tab_sc[2 * QUAD : P, :].bitcast(I32), 0)
        w2_sc_raw = sb([P, PASSES * H], U8, "w2_sc_raw")
        nc.gpsimd.memset(w2_sc_raw[:].bitcast(I32), 0)
        for quad in range(QUADS):
            nc.gpsimd.dma_start(
                out=w2_sc_raw[QUAD * quad : QUAD * quad + QUAD_ROWS, :]
                .bitcast(I32)
                .rearrange("i (a c) -> i a c", a=PASSES),
                in_=w2_scales[:, QUAD_ROWS * quad : QUAD_ROWS * (quad + 1), :].bitcast(I32).rearrange("a i c -> i a c"),
            )
        planes = []
        for a in range(PASSES):
            planes.append(sb([P, S], U8, f"plane{a}"))
            nc.vector.memset(planes[a][:].bitcast(I32), 0)

        tab = {}
        raw = {}

        def load_table(a, at):
            tab[a] = sb([P, T], U32, f"tab{a}", at)
            nc.sync.dma_start(
                out=tab[a][:].bitcast(I32), in_=tab_words[a].rearrange("p t i -> p (t i)").bitcast(I32)
            )

        def load_weight(name, w, a, at):
            raw[name, a] = sb([P, PACK, H], F32, f"{name}_raw{a}", at)
            nc.sync.dma_start(
                out=raw[name, a][:],
                in_=w[a * P * PACK : (a + 1) * P * PACK, :].rearrange("(p j) r -> p j r", j=PACK),
            )

        nc.sync.dma_start(offs_sb[:], offs)
        nc.sync.dma_start(
            out=tab_sc[0 : PASSES * PASS_ROWS, :].bitcast(I32),
            in_=tab_scales.rearrange("a q t -> (a q) t").bitcast(I32),
        )
        load_table(0, TAB0_AT)
        w2_raw = sb([P, PASSES * 2 * H], U8, "w2_raw")
        nc.sync.dma_start(
            out=w2_raw[:].bitcast(I32).rearrange("p (a c) -> p a c", a=PASSES),
            in_=w2_words.bitcast(I32).rearrange("a p c -> p a c"),
        )
        load_table(1, TAB1_AT)
        nc.sync.dma_start(pos2_sb[:], pos2)
        nc.sync.dma_start(pos1_sb[:], pos1)

        v_sc = sb([P, S], U8, "v_sc")
        nc.vector.tensor_copy(out=v_sc[:], in_=tab_sc[:].indirect(offs_sb[:]))
        for a, queue in enumerate((nc.scalar, nc.gpsimd)):
            for i in range(QUAD_ROWS):
                queue.dma_start(
                    out=planes[a][i:P:QUAD, :].bitcast(I32),
                    in_=v_sc[PASS_ROWS * a + i : PASS_ROWS * (a + 1) : QUAD_ROWS, :].bitcast(I32),
                )

        v = {}
        v0 = sb([P, S], U32, "v0")
        nc.vector.tensor_copy(out=v0[:], in_=tab[0][:].indirect(offs_sb[:]))
        load_weight("w3", w3, 0, EARLY_RAW_AT)
        load_weight("w3", w3, 1, LATE_RAW_AT)

        w2_sc = sb([P, PASSES * H], U8, "w2_sc", W2_SC_AT)
        nc.vector.tensor_copy(
            out=w2_sc[:].bitcast(I32).rearrange("p (a t q) -> p a t q", a=PASSES, t=PACK),
            in_=w2_sc_raw[:].bitcast(I32).rearrange("p (a q t) -> p a t q", a=PASSES, t=PACK),
        )
        w2_codes = sb([P, PASSES * 2 * H], U8, "w2_codes", W2_CODES_AT)
        nc.vector.tensor_copy(
            out=w2_codes[:].bitcast(I32).rearrange("p (a t q two) -> p a t q two", a=PASSES, t=PACK, two=2),
            in_=w2_raw[:].bitcast(I32).rearrange("p (a q t two) -> p a t q two", a=PASSES, t=PACK, two=2),
        )

        half_cols = BANK // LIST_ROWS
        for half in range(HALVES):
            v[0, half] = v0[:, half * BANK : (half + 1) * BANK]
            v1 = sb([P, BANK], U32, f"v1_{half}")
            nc.vector.tensor_copy(
                out=v1[:], in_=tab[1][:].indirect(offs_sb[:, half * half_cols : (half + 1) * half_cols])
            )
            v[1, half] = v1[:]
        load_weight("w1", w1, 0, TAB1_AT)

        def first_stage(name, operands, t, half, order):
            acc = bank(f"{name}_{t}_{half}")
            for a in order:
                codes, scales = operands[a, t]
                nc.tensor.matmul_mx(
                    out=acc[:],
                    lhsT=codes,
                    lhsT_scale=scales,
                    rhs=v[a, half].bitcast(FP8X4),
                    rhs_scale=planes[a][:, half * BANK : (half + 1) * BANK],
                    start=(a == order[0]),
                    stop=(a == order[-1]),
                )
            return acc

        def round_weight(name, a, slots, copy, over=None):
            n = len(slots)
            grouped = sb([P, n * P * PACK], BF16, f"{name}_bf{a}_{slots[0]}", over)
            copy(
                out=grouped[:].rearrange("p (t q e j) -> p t q j e", t=n, e=RUN, j=PACK),
                in_=raw[name, a][:].rearrange("p j (q t e) -> p t q j e", t=PACK, e=RUN)[
                    :, slots[0] : slots[0] + n
                ],
            )
            return grouped

        def quantise(name, grouped, over=None):
            width = grouped.shape[1] // PACK
            codes = sb([P, width], U32, f"{name}_codes", over)
            scales = sb([P, width], U8, f"{name}_scales")
            nc.vector.quantize_mx(out=codes[:].bitcast(FP8X4), scales=scales[:], in_=grouped[:])
            return codes, scales

        def quantise_weight(name, a, slots, grouped, operands, over=None):
            codes, scales = quantise(f"{name}_{a}_{slots[0]}", grouped, over)
            for i, t in enumerate(slots):
                operands[a, t] = (
                    codes[:, i * P : (i + 1) * P].bitcast(FP8X4),
                    scales[:, i * P : (i + 1) * P],
                )

        w2_ops = {}
        for a in range(PASSES):
            for t in range(PACK):
                c0 = a * H + t * P
                w2_ops[a, t] = (w2_codes[:, 2 * c0 : 2 * (c0 + P)].bitcast(FP4X4), w2_sc[:, c0 : c0 + P])
        tanh = {}
        tanh_over = {(PACK - 1, HALVES - 1): LAST_TANH_AT}
        for half in range(HALVES):
            for t in range(PACK):
                acc = first_stage("tone", w2_ops, t, half, [0, 1])
                tanh[t, half] = sb([P, BANK], F32, f"tanh_{t}_{half}", tanh_over.get((t, half)))
                nc.scalar.activation(out=tanh[t, half][:], in_=acc[:], func=ACT.Tanh)

        late_first = [1, 0]
        every = list(range(PACK))
        w3_ops = {}
        w3_early = round_weight("w3", 0, every, nc.vector.tensor_copy, TAB1_AT + RAW_BYTES)
        load_weight("w1", w1, 1, EARLY_RAW_AT)
        quantise_weight("w3", 0, every, w3_early, w3_ops)
        for slots in (every[:2], every[2:]):
            quantise_weight("w3", 1, slots, round_weight("w3", 1, slots, nc.vector.tensor_copy), w3_ops)
        u = {}
        u_over = {(0, 0): X2_AT, (1, 0): PICK2_AT}
        for half in range(HALVES):
            for t in range(PACK):
                acc = first_stage("image", w3_ops, t, half, late_first)
                u[t, half] = sb([P, BANK], F32, f"u_{t}_{half}", u_over.get((t, half)))
                nc.vector.tensor_tensor(out=u[t, half][:], in0=acc[:], in1=tanh[t, half][:], op=ALU.add)

        gain_sb = sb([P, PACK], F32, "gain_sb", TAB1_AT - 128)
        cap_sb = sb([P, BLOCKS], F32, "cap_sb", TAB1_AT - 64)
        with nc.allow_non_contiguous_dma(reason="one value a partition and slot"):
            for e in range(RUN):
                nc.sync.dma_start(out=gain_sb[e:P:RUN, :], in_=gain.rearrange("(q t e) -> e q t", t=PACK, e=RUN)[e])
            nc.sync.dma_start(out=cap_sb[:], in_=cap.rearrange("(b p) -> p b", p=P))

        sign_sb = sb([P, PACK], F32, "sign_sb")
        nc.gpsimd.tensor_scalar(
            out=sign_sb[:], in0=gain_sb[:], scalar1=0.0, scalar2=2.0, op0=ALU.is_ge, op1=ALU.mult
        )
        nc.gpsimd.tensor_scalar(
            out=sign_sb[:], in0=sign_sb[:], scalar1=-1.0, scalar2=1.0, op0=ALU.add, op1=ALU.mult
        )

        w1_ops = {}
        w1_early = round_weight("w1", 0, every, nc.scalar.copy, W2_CODES_AT)
        quantise_weight("w1", 0, every, w1_early, w1_ops, "tanh_1_1")
        w1_late = {t: round_weight("w1", 1, [t], nc.scalar.copy) for t in (0, 1, 3, 2)}
        quantise_weight("w1", 1, [0], w1_late[0], w1_ops, "tanh_2_1")
        quantise_weight("w1", 1, [1], w1_late[1], w1_ops, LAST_TANH_AT)
        quantise_weight("w1", 1, [3], w1_late[3], w1_ops, LAST_TANH_AT + 4 * P)

        h = [sb([P, S], F32, f"h{t}") for t in range(PACK)]

        def product_on_vector(t):
            for half in range(HALVES):
                acc = first_stage("theme", w1_ops, t, half, late_first)
                nc.vector.scalar_tensor_tensor(
                    out=h[t][:, half * BANK : (half + 1) * BANK],
                    in0=acc[:],
                    scalar=sign_sb[:, t : t + 1],
                    in1=u[t, half][:],
                    op0=ALU.mult,
                    op1=ALU.mult,
                )

        picked1 = sb([P, PACK, PICK], F32, "picked1")

        def product_on_gpsimd(t, staging):
            for half in range(HALVES):
                acc = first_stage("theme", w1_ops, t, half, late_first)
                nc.scalar.activation(out=staging[half], in_=acc[:], func=ACT.Copy, scale=sign_sb[:, t : t + 1])
                nc.gpsimd.tensor_tensor(
                    out=h[t][:, half * BANK : (half + 1) * BANK], in0=staging[half], in1=u[t, half][:], op=ALU.mult
                )

        def pick2(t, over=None):
            picked2 = sb([P, PICK], F32, f"picked2_{t}", over)
            nc.vector.tensor_copy(out=picked2[:], in_=h[t][:].indirect(pos2_sb[:]))
            nc.scalar.activation(
                out=x2_pairs[:].rearrange("p (pair j side) -> p pair side j", pair=2, side=2)[:, t // 2, t % 2, :],
                in_=picked2[:],
                func=ACT.Abs,
                scale=gain_sb[:, t : t + 1],
            )

        def pick1(t, pieces):
            width = PICK // pieces
            for i in range(pieces):
                nc.vector.tensor_copy(
                    out=picked1[:, t, i * width : (i + 1) * width],
                    in_=h[t][:].indirect(pos1_sb[:, i * width // LIST_ROWS : (i + 1) * width // LIST_ROWS]),
                )

        product_on_vector(0)
        quantise_weight("w1", 1, [2], w1_late[2], w1_ops, X2_AT)
        product_on_gpsimd(3, [sb([P, BANK], F32, "theme3")[:], picked1[:, 1, :]])
        product_on_gpsimd(2, [sb([P, BANK], F32, "theme2")[:], picked1[:, 3, :]])
        x2_pairs = sb([P, PICK * PACK], BF16, "x2_pairs", X2_AT)
        pick2(0)
        product_on_vector(1)
        pick2(1)
        pick1(0, 1)
        pick2(3, PICK2_AT)
        pick1(1, 1)
        pick2(2)
        x2_bf = sb([P, PICK * PACK], BF16, "x2_bf")
        nc.scalar.copy(
            out=x2_bf[:].bitcast(U32).rearrange("p (j pair) -> p j pair", pair=2),
            in_=x2_pairs[:].bitcast(U32).rearrange("p (pair j) -> p j pair", pair=2),
        )
        pick1(3, 1)
        pick1(2, BLOCKS)

        x1_bf = []
        for b in range(BLOCKS):
            x1_bf.append(sb([P, P * PACK], BF16, f"x1_bf{b}"))
            nc.scalar.copy(
                out=x1_bf[b][:].rearrange("p (c i t) -> p c t i", i=RUN, t=PACK),
                in_=picked1[:, :, b * P : (b + 1) * P].rearrange("p t (c i) -> p c t i", i=RUN),
            )

        x2_codes, x2_scales = quantise("x2", x2_bf)
        scores = {}

        def score(b):
            x1_codes, x1_scales = quantise(f"x1_{b}", x1_bf[b])
            scores[b] = bank(f"e_{b}")
            nc.tensor.matmul_mx(
                out=scores[b][:],
                lhsT=x1_codes[:].bitcast(FP8X4),
                lhsT_scale=x1_scales[:],
                rhs=x2_codes[:].bitcast(FP8X4),
                rhs_scale=x2_scales[:],
                start=True,
                stop=True,
            )

        def finish(b, queues):
            width = PICK // len(queues)
            for i, queue in enumerate(queues):
                span = slice(i * width, (i + 1) * width)
                capped = sb([P, width], F32, f"capped{b}_{i}")
                nc.vector.tensor_scalar(
                    out=capped[:], in0=scores[b][:, span], scalar1=cap_sb[:, b : b + 1], scalar2=None, op0=ALU.min
                )
                nc.scalar.activation(out=capped[:], in_=capped[:], func=ACT.Exp)
                queue.dma_start(out=out[b * P : (b + 1) * P, span], in_=capped[:])

        for b in range(BLOCKS - 1):
            score(b)
        finish(0, [nc.sync])
        score(BLOCKS - 1)
        for b in range(1, BLOCKS - 1):
            finish(b, [nc.sync])
        finish(BLOCKS - 1, [nc.sync, nc.scalar])
